import numpy as np
import ml_dtypes


def mxq(x, axis, fmt="e4m3"):
    dtype, down = {"e4m3": (ml_dtypes.float8_e4m3fn, 7), "e5m2": (ml_dtypes.float8_e5m2, 14)}[fmt]
    v = np.moveaxis(np.asarray(x, np.float32).astype(ml_dtypes.bfloat16).astype(np.float64), axis, -1)
    blocks = v.reshape(v.shape[:-1] + (-1, 32))
    amax = np.abs(blocks).max(-1, keepdims=True)
    byte = np.maximum(np.where(amax > 0, np.frexp(amax)[1] - 1 + 127, 0) - down, 1)
    scale = np.exp2(byte - 127.0)
    codes = (blocks / scale).astype(np.float32).astype(dtype).astype(np.float64)
    return np.moveaxis((codes * scale).reshape(v.shape), -1, axis)


WIDE = False


def mx_kscale(k):
    if not WIDE:
        return np.ones(k)
    levels = np.array([10, -10, 5, -5, 0])
    if k % 512:
        return np.exp2(np.random.permutation(np.resize(levels, k // 32))).repeat(32)
    a = np.empty((k // 512, 16))
    for p in range(k // 512):
        a[p, :8] = np.random.permutation(np.resize(levels, 8))
        for g in range(8):
            far = levels[np.abs(levels - a[p, g]) >= 10]
            a[p, g + 8] = far[np.random.randint(len(far))]
    return np.exp2(a.ravel()).repeat(32)


def f64(x):
    return np.asarray(x).astype(np.float64)


def striped(idx):
    return np.tile(idx.reshape(-1, 16).T, (8, 1)).astype(np.uint16)


def unstriped(offs):
    return offs[:16].T.reshape(-1).astype(np.int64)


def pack_weight(w):
    k, n = w.shape
    w = f64(np.asarray(w, np.float32).astype(ml_dtypes.bfloat16)).reshape(k // 32, 32, n)
    amax = np.abs(w).max(1)
    byte = np.clip(np.where(amax > 0, np.frexp(amax)[1] - 1 + 127 - 7, 1), 1, 254)
    scaled = (w * np.exp2(127.0 - byte)[:, None, :]).reshape(k, n).astype(np.float32)
    words = np.ascontiguousarray(scaled.reshape(k // 512, 128, 4, n).transpose(0, 1, 3, 2)).astype(ml_dtypes.float8_e4m3fn).view(np.uint8)
    return words, np.ascontiguousarray(byte.astype(np.uint8).reshape(k // 512, 16, n))


def unpack_weight(words, scales):
    g, p, n, _ = words.shape
    vals = np.ascontiguousarray(words).view(ml_dtypes.float8_e4m3fn).astype(np.float64) * np.repeat(np.exp2(scales.astype(np.float64) - 127.0), 8, axis=1)[..., None]
    return vals.transpose(0, 1, 3, 2).reshape(g * 512, n)


def planes(y):
    n, m = y.shape
    v = y.astype(np.float32).astype(ml_dtypes.bfloat16).astype(np.float64).reshape(n // 32, 32, m)
    top = np.abs(v).max(1)
    byte = np.clip(np.where(top > 0, np.frexp(top)[1] - 1 + 127 - 7, 1), 1, 254)
    codes = (v * np.exp2(127.0 - byte)[:, None, :]).reshape(n, m).astype(np.float32).astype(ml_dtypes.float8_e4m3fn).view(np.uint8)
    words = codes.reshape(n // 512, 128, 4, m).transpose(0, 1, 3, 2)
    return np.ascontiguousarray(words), np.ascontiguousarray(byte.astype(np.uint8).reshape(n // 512, 16, m))


def sigmoid(v):
    return 1.0 / (1.0 + np.exp(-np.maximum(v, -700.0)))


K, T, S, V, N = 512, 1024, 512, 256, 512


def setup_inputs():
    n = np.random.standard_normal
    s = mx_kscale(K)[:, None]
    near = np.random.permutation(S)
    packed_xT = pack_weight(n((K, T)) * s)
    return {
        "x_words": packed_xT[0],
        "x_scales": packed_xT[1],
        "eT": (n((K, V)) * s).astype(np.float32),
        "w1": (n((K, N)) / np.sqrt(2 * K) / s).astype(np.float32),
        "w2": (n((K, N)) / np.sqrt(2 * K) / s).astype(np.float32),
        "w3": (n((K, N)) / np.sqrt(2 * K) / s).astype(np.float32),
        "v1": (n((K, N)) / np.sqrt(2 * K) / s).astype(np.float32),
        "v2": (n((K, N)) / np.sqrt(2 * K) / s).astype(np.float32),
        "v3": (n((K, N)) / np.sqrt(2 * K) / s).astype(np.float32),
        "cell": (n((N, S))).astype(np.float32),
        "offs": striped(np.random.permutation(T)[:S]),
        "pos1": striped(near[:V]),
        "pos2": striped(near[V:]),
    }


def reference(x_words, x_scales, eT, w1, w2, w3, v1, v2, v3, cell, offs, pos1, pos2):
    eTq = mxq(f64(eT), 0, "e4m3")
    e1 = mxq(f64(w1), 0, "e4m3").T @ eTq
    xq = unpack_weight(x_words, x_scales)[:, unstriped(offs)]
    h1 = mxq(f64(v1), 0, "e4m3").T @ xq
    a = sigmoid(e1 + h1[:, unstriped(pos1)] + h1[:, unstriped(pos2)])
    e2 = mxq(f64(w2), 0, "e4m3").T @ eTq
    h2 = mxq(f64(v2), 0, "e4m3").T @ xq
    g = np.tanh(e2 + h2[:, unstriped(pos1)] + h2[:, unstriped(pos2)])
    e3 = mxq(f64(w3), 0, "e4m3").T @ eTq
    h3 = mxq(f64(v3), 0, "e4m3").T @ xq
    out_0 = a * g + (sigmoid(e3 + h3[:, unstriped(pos1)])) * f64(cell)[:, unstriped(pos1)] + (sigmoid(e3 + h3[:, unstriped(pos2)])) * f64(cell)[:, unstriped(pos2)]
    return (out_0,) + planes(out_0)

@@ -1,0 +1,309 @@
+from contextlib import ExitStack
+
+import concourse.mybir as mybir
+from concourse.masks import make_identity
+
+F32 = mybir.dt.float32
+BF16 = mybir.dt.bfloat16
+I32 = mybir.dt.int32
+U32 = mybir.dt.uint32
+U16 = mybir.dt.uint16
+U8 = mybir.dt.uint8
+FP8X4 = mybir.dt.float8_e4m3fn_x4
+ACT = mybir.ActivationFunctionType
+ALU = mybir.AluOpType
+
+K, T, S, V, N = 512, 1024, 512, 256, 512
+P = 128
+PACK = 4
+HALF = 256
+FLOPS = 2 * K * N * 3 * (S + V)
+
+
+def tile_picked_ztree_cell_po_kernel(
+    tc, x_words, x_scales, eT, w1, w2, w3, v1, v2, v3, cell, offs, pos1, pos2, out_0, out_1, out_2
+):
+    nc = tc.nc
+    with ExitStack() as ctx:
+        keep = ctx.enter_context(tc.tile_pool(name="keep", bufs=1))
+        mm = ctx.enter_context(tc.psum_pool(name="mm", bufs=2))
+        held = ctx.enter_context(tc.psum_pool(name="held", bufs=1))
+
+        def sb(name, shape, dtype, tag=None):
+            return keep.tile(shape, dtype, name=name, tag=tag or name, align_bytes=64)
+
+        offs_sb = keep.tile([P, S // 16], U16, name="offs_sb")
+        pos_sb = [keep.tile([P, V // 16], U16, name="pos_sb%d" % d) for d in range(2)]
+
+        xs_all = sb("xs_all", [P, T], U8)
+        nc.gpsimd.memset(xs_all[:].bitcast(I32), 0)
+        warm = sb("warm", [P, 16], F32)
+        nc.gpsimd.memset(warm[:, 0:8], 0.0)
+        for q in range(4):
+            nc.scalar.dma_start(
+                out=xs_all[32 * q : 32 * q + 4, :].bitcast(I32), in_=x_scales[0, 4 * q : 4 * q + 4, :].bitcast(I32)
+            )
+        nc.scalar.activation(warm[:, 8:16], warm[:, 0:8], ACT.Sigmoid)
+        ident = sb("ident", [P, P], F32)
+        make_identity(nc, ident[:])
+
+        cell_sb = [sb("cell%d" % t, [P, S], F32) for t in range(PACK)]
+        cell_rows = cell.rearrange("(p t) s -> p t s", t=PACK)
+        xw_all = sb("xw_all", [P, T], I32)
+
+        raws = {}
+
+        def load(name, src, c0, c1):
+            raw = sb("raw_%s_%d" % (name, c0), [P, PACK, c1 - c0], F32)
+            nc.sync.dma_start(out=raw[:], in_=src.rearrange("(p j) c -> p j c", j=PACK)[:, :, c0:c1])
+            for c in range(c0, c1, HALF):
+                raws[(name, c // HALF)] = raw[:, :, c - c0 : c - c0 + HALF]
+
+        nc.sync.dma_start(offs_sb[:], offs)
+        nc.sync.dma_start(out=xw_all[:], in_=x_words[0].rearrange("p c r -> p (c r)").bitcast(I32))
+        load("v1", v1, 0, HALF)
+        load("v1", v1, HALF, N)
+        nc.sync.dma_start(pos_sb[0][:], pos1)
+        nc.sync.dma_start(pos_sb[1][:], pos2)
+        load("v2", v2, 0, HALF)
+        load("v2", v2, HALF, N)
+        load("v3", v3, 0, N)
+        load("eT", eT, 0, V)
+        for name, src in (("w3", w3), ("w1", w1), ("w2", w2)):
+            load(name, src, 0, N)
+        for t in range(PACK):
+            nc.sync.dma_start(out=cell_sb[t][:], in_=cell_rows[:, t, :])
+
+        slot = {
+            ("v3", 0): "h_v1_0",
+            ("eT", 0): "h_v1_1",
+            ("w3", 0): "h_v1_3",
+            ("w1", 0): "h_v2_0",
+            ("w1", 1): "h_v2_2",
+            ("w2", 0): "h_v2_3",
+            ("w2", 1): "h_v3_0",
+        }
+        staged = {}
+        codes = {}
+
+        def cast(engine, dst, src):
+            if engine == "g":
+                nc.gpsimd.tensor_scalar(dst, src, 1.0, 0.0, ALU.mult, ALU.add)
+            elif engine == "v":
+                nc.vector.tensor_copy(out=dst, in_=src)
+            else:
+                nc.scalar.copy(out=dst, in_=src)
+
+        def prepare(name, half, engine):
+            raw = raws[(name, half)]
+            pieces = 2 if engine == "g" else 1
+            width = HALF // pieces
+            if name in ("v3", "w3"):
+                if (name, 0) not in staged:
+                    both = sb("bf_" + name, [P, PACK, P, PACK], BF16, tag=slot.get((name, 0)))
+                    for u in range(2):
+                        staged[(name, u)] = both[:, 2 * u : 2 * u + 2, :, :].rearrange("p t m j -> p (t m j)")
+                    staged[name] = both
+                for c in range(0, HALF, width):
+                    m0 = (HALF * half + c) // PACK
+                    cast(
+                        engine,
+                        staged[name][:, :, m0 : m0 + width // PACK, :].rearrange("p t m j -> p m t j"),
+                        raw[:, :, c : c + width].rearrange("p j (m t) -> p m t j", t=PACK),
+                    )
+            else:
+                bf = sb("bf_%s_%d" % (name, half), [P, HALF, PACK], BF16, tag=slot.get((name, half)))
+                staged[(name, half)] = bf[:].rearrange("p c j -> p (c j)")
+                for c in range(0, HALF, width):
+                    if engine == "g":
+                        cast(engine, bf[:, c : c + width, :], raw[:, :, c : c + width].rearrange("p j c -> p c j"))
+                    else:
+                        cast(
+                            engine,
+                            bf[:].rearrange("p (c i) j -> p c j i", i=4),
+                            raw.rearrange("p j (c i) -> p c j i", i=4),
+                        )
+
+        def quantize(name, half):
+            cw = sb("cw_%s_%d" % (name, half), [P, HALF], U32)
+            cs = sb("cs_%s_%d" % (name, half), [P, HALF], U8)
+            nc.vector.quantize_mx(out=cw[:].bitcast(FP8X4), scales=cs[:], in_=staged[(name, half)])
+            codes[(name, half)] = (cw, cs)
+
+        xw = sb("xw", [P, S], U32)
+        xs = sb("xs", [P, S], U8)
+
+        def product(out, name, i, moving, moving_scale):
+            cw, cs = codes[(name, i // 2)]
+            cols = slice(P * (i % 2), P * (i % 2) + P)
+            nc.tensor.matmul_mx(
+                out=out,
+                lhsT=cw[:, cols].bitcast(FP8X4),
+                lhsT_scale=cs[:, cols],
+                rhs=moving.bitcast(FP8X4),
+                rhs_scale=moving_scale,
+                start=True,
+                stop=True,
+            )
+
+        def child_half(name, half):
+            quantize(name, half)
+            hs = []
+            for i in (2 * half, 2 * half + 1):
+                acc = mm.tile([P, S], F32, name="acc")
+                product(acc[:], name, i, xw[:], xs[:])
+                h = sb("h_%s_%d" % (name, i), [P, S], F32)
+                nc.scalar.copy(out=h[:], in_=acc[:])
+                hs.append(h)
+            return hs
+
+        def node_half(name, half):
+            quantize(name, half)
+            acc = mm.tile([P, S], F32, name="acc")
+            ew, es = codes[("eT", 0)]
+            for u in range(2):
+                product(acc[:, V * u : V * u + V], name, 2 * half + u, ew[:], es[:])
+            e = sb("e_%s_%d" % (name, half), [P, 2, V], F32)
+            nc.scalar.copy(out=e[:].rearrange("p u v -> p (u v)"), in_=acc[:])
+            return [e[:, 0, :], e[:, 1, :]]
+
+        def turn(bank, i, block, start, stop):
+            nc.tensor.matmul(bank[:, P * i : P * i + P], block, ident[:], start=start, stop=stop, is_transpose=True)
+
+        def tag_of(after):
+            return after and (slot.get(after) or "bf_%s_%d" % after)
+
+        def gather_turn(name, banks, i, window, after=None):
+            got = sb("u_%s_%d" % (name, i), [P, 2, V], F32, tag=tag_of(after))
+            for d in range(2):
+                nc.vector.tensor_copy(got[:, d, :], window[:].indirect(pos_sb[d][:]))
+            for d in range(2):
+                for hv in range(2):
+                    turn(banks[hv], i, got[:, d, P * hv : P * hv + P], i == 0 and d == 0, False)
+
+        def close(name, banks, e, func):
+            res = []
+            for hv in range(2):
+                for i in range(PACK):
+                    turn(banks[hv], i, e[i][:, P * hv : P * hv + P], False, i == PACK - 1)
+                gate = sb("%s%d" % (name, hv), [P, N], F32)
+                nc.scalar.activation(
+                    gate[:].rearrange("v (t p) -> v t p", t=PACK),
+                    banks[hv][:].rearrange("v (p t) -> v t p", t=PACK),
+                    func,
+                )
+                res.append(gate)
+            return res
+
+        def forget(t, window, e, after=None):
+            pre = sb("pre_f%d" % t, [P, 2, V], F32, tag=tag_of(after))
+            for d in range(2):
+                nc.vector.tensor_tensor(pre[:, d, :], window[:].indirect(pos_sb[d][:]), e, ALU.add)
+            return pre
+
+        def squash(t, pre):
+            f = sb("f%d" % t, [P, 2, V], F32)
+            nc.scalar.activation(f[:].rearrange("p d v -> p (d v)"), pre[:].rearrange("p d v -> p (d v)"), ACT.Sigmoid)
+            return f
+
+        pre_a = [held.tile([P, N], F32, name="pre_a%d" % hv) for hv in range(2)]
+        pre_g = [held.tile([P, N], F32, name="pre_g%d" % hv) for hv in range(2)]
+        total = [held.tile([P, N], F32, name="total%d" % hv) for hv in range(2)]
+        eng = {"v1": "vs", "v2": "vs", "v3": "sv", "eT": "s", "w3": "sv", "w1": "ss", "w2": "ss"}
+
+        nc.vector.tensor_copy(xs[:], xs_all[:].indirect(offs_sb[:]))
+        nc.vector.tensor_copy(xw[:], xw_all[:].bitcast(U32).indirect(offs_sb[:]))
+        prepare("v1", 0, eng["v1"][0])
+        prepare("v1", 1, eng["v1"][1])
+        h1 = child_half("v1", 0)
+        h1 = h1 + child_half("v1", 1)
+        prepare("v2", 0, eng["v2"][0])
+        prepare("v2", 1, eng["v2"][1])
+        gather_turn("v1", pre_a, 0, h1[0])
+        h2 = child_half("v2", 0)
+        gather_turn("v1", pre_a, 1, h1[1], after=("v2", 0))
+        prepare("v3", 0, eng["v3"][0])
+        h2 = h2 + child_half("v2", 1)
+        gather_turn("v1", pre_a, 2, h1[2], after=("v2", 1))
+        prepare("v3", 1, eng["v3"][1])
+        prepare("eT", 0, eng["eT"][0])
+        gather_turn("v1", pre_a, 3, h1[3])
+        prepare("w3", 0, eng["w3"][0])
+        h3 = child_half("v3", 0) + child_half("v3", 1)
+        gather_turn("v2", pre_g, 0, h2[0], after=("v3", 0))
+        quantize("eT", 0)
+        gather_turn("v2", pre_g, 1, h2[1], after=("eT", 0))
+        prepare("w3", 1, eng["w3"][1])
+        prepare("w1", 0, eng["w1"][0])
+        e3 = node_half("w3", 0) + node_half("w3", 1)
+        gather_turn("v2", pre_g, 2, h2[2], after=("w3", 0))
+        prepare("w1", 1, eng["w1"][1])
+        e1 = node_half("w1", 0)
+        gather_turn("v2", pre_g, 3, h2[3], after=("w1", 0))
+        prepare("w2", 0, eng["w2"][0])
+        e1 = e1 + node_half("w1", 1)
+        pre = [forget(0, h3[0], e3[0], after=("w1", 1))]
+        prepare("w2", 1, eng["w2"][1])
+        pre.append(forget(1, h3[1], e3[1]))
+        e2 = node_half("w2", 0)
+        pre.append(forget(2, h3[2], e3[2], after=("w2", 0)))
+        e2 = e2 + node_half("w2", 1)
+        pre.append(forget(3, h3[3], e3[3], after=("w2", 1)))
+        f = [squash(t, pre[t]) for t in range(PACK)]
+        a = close("a", pre_a, e1, ACT.Sigmoid)
+        g = close("g", pre_g, e2, ACT.Tanh)
+
+        fc0 = sb("fc0", [P, PACK, V], F32)
+        for t in range(PACK):
+            nc.vector.tensor_tensor(fc0[:, t, :], cell_sb[t][:].indirect(pos_sb[0][:]), f[t][:, 0, :], ALU.mult)
+        for hv in range(2):
+            ag = sb("ag%d" % hv, [P, N], F32)
+            nc.vector.tensor_tensor(ag[:], a[hv][:], g[hv][:], ALU.mult)
+            for t in range(PACK):
+                turn(total[hv], t, ag[:, P * t : P * t + P], t == 0, False)
+        for hv in range(2):
+            bank = held.tile([P, N], F32, name="turned_fc%d" % hv, tag="pre_a%d" % hv)
+            for t in range(PACK):
+                turn(bank, t, fc0[:, t, P * hv : P * hv + P], True, True)
+            turned = sb("turned%d" % hv, [P, N], F32)
+            nc.scalar.copy(out=turned[:], in_=bank[:])
+            for t in range(PACK):
+                turn(total[hv], t, turned[:, P * t : P * t + P], False, t == PACK - 1)
+
+        y_codes = sb("y_codes", [P, V], U32)
+        y_scales = sb("y_scales", [P, V], U8)
+        out_rows = out_0.rearrange("(p t) v -> p t v", t=PACK)
+        out_words = out_1[0].rearrange("p c r -> p (c r)").bitcast(I32)
+        fc1 = []
+        for hv in range(2):
+            piece = sb("fc1_%d" % hv, [P, PACK, P], F32)
+            for t in range(PACK):
+                nc.vector.tensor_tensor(
+                    piece[:, t, :],
+                    cell_sb[t][:].indirect(pos_sb[1][:, 8 * hv : 8 * hv + 8]),
+                    f[t][:, 1, P * hv : P * hv + P],
+                    ALU.mult,
+                )
+            fc1.append(piece)
+        for hv in range(2):
+            cols = slice(P * hv, P * hv + P)
+            y = sb("y%d" % hv, [P, PACK, P], F32)
+            nc.vector.tensor_tensor(
+                y[:].rearrange("p t v -> p (t v)"), total[hv][:], fc1[hv][:].rearrange("p t v -> p (t v)"), ALU.add
+            )
+            nc.sync.dma_start(out=out_rows[:, :, cols], in_=y[:])
+            y_bf = sb("y_bf%d" % hv, [P, P, PACK], BF16)
+            cast(
+                "sv"[hv],
+                y_bf[:].rearrange("p (c i) t -> p c t i", i=4),
+                y[:].rearrange("p t (c i) -> p c t i", i=4),
+            )
+            nc.vector.quantize_mx(
+                out=y_codes[:, cols].bitcast(FP8X4), scales=y_scales[:, cols], in_=y_bf[:].rearrange("p v t -> p (v t)")
+            )
+            nc.sync.dma_start(out=out_words[:, cols], in_=y_codes[:, cols].bitcast(I32))
+        for q in range(4):
+            queue = nc.sync if q % 2 == 0 else nc.scalar
+            queue.dma_start(
+                out=out_2[0, 4 * q : 4 * q + 4, :].bitcast(I32), in_=y_scales[32 * q : 32 * q + 4, :].bitcast(I32)
+            )

@@ -39,10 +39,6 @@ def tile_picked_ztree_cell_po_kernel(
         nc.gpsimd.memset(xs_all[:].bitcast(I32), 0)
         warm = sb("warm", [P, 16], F32)
         nc.gpsimd.memset(warm[:, 0:8], 0.0)
-        for q in range(4):
-            nc.scalar.dma_start(
-                out=xs_all[32 * q : 32 * q + 4, :].bitcast(I32), in_=x_scales[0, 4 * q : 4 * q + 4, :].bitcast(I32)
-            )
         nc.scalar.activation(warm[:, 8:16], warm[:, 0:8], ACT.Sigmoid)
         ident = sb("ident", [P, P], F32)
         make_identity(nc, ident[:])
@@ -61,28 +57,32 @@ def tile_picked_ztree_cell_po_kernel(
 
         nc.sync.dma_start(offs_sb[:], offs)
         nc.sync.dma_start(out=xw_all[:], in_=x_words[0].rearrange("p c r -> p (c r)").bitcast(I32))
+        for q in range(4):
+            nc.sync.dma_start(
+                out=xs_all[32 * q : 32 * q + 4, :].bitcast(I32), in_=x_scales[0, 4 * q : 4 * q + 4, :].bitcast(I32)
+            )
         load("v1", v1, 0, HALF)
         load("v1", v1, HALF, N)
         nc.sync.dma_start(pos_sb[0][:], pos1)
         nc.sync.dma_start(pos_sb[1][:], pos2)
         load("v2", v2, 0, HALF)
         load("v2", v2, HALF, N)
-        load("v3", v3, 0, N)
         load("eT", eT, 0, V)
-        for name, src in (("w3", w3), ("w1", w1), ("w2", w2)):
+        for name, src in (("w1", w1), ("v3", v3), ("w3", w3), ("w2", w2)):
             load(name, src, 0, N)
         for t in range(PACK):
             nc.sync.dma_start(out=cell_sb[t][:], in_=cell_rows[:, t, :])
 
         slot = {
-            ("v3", 0): "h_v1_0",
-            ("eT", 0): "h_v1_1",
-            ("w3", 0): "h_v1_3",
-            ("w1", 0): "h_v2_0",
-            ("w1", 1): "h_v2_2",
-            ("w2", 0): "h_v2_3",
-            ("w2", 1): "h_v3_0",
+            ("v2", 0): "bf_v1_1",
+            ("w1", 0): "h_v1_0",
+            ("w1", 1): "h_v1_1",
+            ("v3", 0): "h_v1_2",
+            ("w3", 0): "h_v2_0",
+            ("w2", 0): "u_v2_1",
+            ("w2", 1): "u_v2_2",
         }
+        window_slot = {("v2", 2): "raw_v3_0", ("v2", 3): "raw_w3_0"}
         staged = {}
         codes = {}
 
@@ -108,8 +108,8 @@ def tile_picked_ztree_cell_po_kernel(
                     m0 = (HALF * half + c) // PACK
                     cast(
                         engine,
-                        staged[name][:, :, m0 : m0 + width // PACK, :].rearrange("p t m j -> p m t j"),
-                        raw[:, :, c : c + width].rearrange("p j (m t) -> p m t j", t=PACK),
+                        staged[name][:, :, m0 : m0 + width // PACK, :].rearrange("p t m j -> p m j t"),
+                        raw[:, :, c : c + width].rearrange("p j (m t) -> p m j t", t=PACK),
                     )
             else:
                 bf = sb("bf_%s_%d" % (name, half), [P, HALF, PACK], BF16, tag=slot.get((name, half)))
@@ -146,19 +146,14 @@ def tile_picked_ztree_cell_po_kernel(
                 stop=True,
             )
 
-        def child_half(name, half):
-            quantize(name, half)
-            hs = []
-            for i in (2 * half, 2 * half + 1):
-                acc = mm.tile([P, S], F32, name="acc")
-                product(acc[:], name, i, xw[:], xs[:])
-                h = sb("h_%s_%d" % (name, i), [P, S], F32)
-                nc.scalar.copy(out=h[:], in_=acc[:])
-                hs.append(h)
-            return hs
+        def child(name, i):
+            acc = mm.tile([P, S], F32, name="acc")
+            product(acc[:], name, i, xw[:], xs[:])
+            h = sb("h_%s_%d" % (name, i), [P, S], F32, tag=window_slot.get((name, i)))
+            nc.scalar.copy(out=h[:], in_=acc[:])
+            return h
 
         def node_half(name, half):
-            quantize(name, half)
             acc = mm.tile([P, S], F32, name="acc")
             ew, es = codes[("eT", 0)]
             for u in range(2):
@@ -188,8 +183,8 @@ def tile_picked_ztree_cell_po_kernel(
                     turn(banks[hv], i, e[i][:, P * hv : P * hv + P], False, i == PACK - 1)
                 gate = sb("%s%d" % (name, hv), [P, N], F32)
                 nc.scalar.activation(
-                    gate[:].rearrange("v (t p) -> v t p", t=PACK),
-                    banks[hv][:].rearrange("v (p t) -> v t p", t=PACK),
+                    gate[:].rearrange("v (t p) -> v p t", t=PACK),
+                    banks[hv][:].rearrange("v (p t) -> v p t", t=PACK),
                     func,
                 )
                 res.append(gate)
@@ -209,48 +204,65 @@ def tile_picked_ztree_cell_po_kernel(
         pre_a = [held.tile([P, N], F32, name="pre_a%d" % hv) for hv in range(2)]
         pre_g = [held.tile([P, N], F32, name="pre_g%d" % hv) for hv in range(2)]
         total = [held.tile([P, N], F32, name="total%d" % hv) for hv in range(2)]
-        eng = {"v1": "vs", "v2": "vs", "v3": "sv", "eT": "s", "w3": "sv", "w1": "ss", "w2": "ss"}
+        eng = {"v1": "sv", "v2": "vg", "v3": "ss", "eT": "g", "w3": "ss", "w1": "gg", "w2": "gg"}
 
-        nc.vector.tensor_copy(xs[:], xs_all[:].indirect(offs_sb[:]))
         nc.vector.tensor_copy(xw[:], xw_all[:].bitcast(U32).indirect(offs_sb[:]))
+        nc.vector.tensor_copy(xs[:], xs_all[:].indirect(offs_sb[:]))
         prepare("v1", 0, eng["v1"][0])
+        quantize("v1", 0)
+        h1 = [child("v1", 0), child("v1", 1)]
         prepare("v1", 1, eng["v1"][1])
-        h1 = child_half("v1", 0)
-        h1 = h1 + child_half("v1", 1)
+        quantize("v1", 1)
         prepare("v2", 0, eng["v2"][0])
         prepare("v2", 1, eng["v2"][1])
         gather_turn("v1", pre_a, 0, h1[0])
-        h2 = child_half("v2", 0)
-        gather_turn("v1", pre_a, 1, h1[1], after=("v2", 0))
-        prepare("v3", 0, eng["v3"][0])
-        h2 = h2 + child_half("v2", 1)
-        gather_turn("v1", pre_a, 2, h1[2], after=("v2", 1))
-        prepare("v3", 1, eng["v3"][1])
+        quantize("v2", 0)
+        h1 = h1 + [child("v1", 2), child("v1", 3)]
+        gather_turn("v1", pre_a, 1, h1[1])
+        quantize("v2", 1)
         prepare("eT", 0, eng["eT"][0])
-        gather_turn("v1", pre_a, 3, h1[3])
-        prepare("w3", 0, eng["w3"][0])
-        h3 = child_half("v3", 0) + child_half("v3", 1)
-        gather_turn("v2", pre_g, 0, h2[0], after=("v3", 0))
-        quantize("eT", 0)
-        gather_turn("v2", pre_g, 1, h2[1], after=("eT", 0))
-        prepare("w3", 1, eng["w3"][1])
+        h2 = [child("v2", 0)]
+        gather_turn("v1", pre_a, 2, h1[2])
         prepare("w1", 0, eng["w1"][0])
-        e3 = node_half("w3", 0) + node_half("w3", 1)
-        gather_turn("v2", pre_g, 2, h2[2], after=("w3", 0))
+        h2.append(child("v2", 1))
+        gather_turn("v1", pre_a, 3, h1[3])
+        quantize("eT", 0)
         prepare("w1", 1, eng["w1"][1])
-        e1 = node_half("w1", 0)
-        gather_turn("v2", pre_g, 3, h2[3], after=("w1", 0))
+        prepare("v3", 0, eng["v3"][0])
+        prepare("v3", 1, eng["v3"][1])
+        h2.append(child("v2", 2))
+        gather_turn("v2", pre_g, 0, h2[0])
+        quantize("w1", 0)
+        quantize("w1", 1)
+        gather_turn("v2", pre_g, 1, h2[1])
+        prepare("w3", 0, eng["w3"][0])
+        quantize("v3", 0)
+        quantize("v3", 1)
+        prepare("w3", 1, eng["w3"][1])
+        h2.append(child("v2", 3))
+        h3 = [child("v3", 0), child("v3", 1)]
+        gather_turn("v2", pre_g, 2, h2[2])
+        quantize("w3", 0)
+        quantize("w3", 1)
+        e3 = node_half("w3", 0)
         prepare("w2", 0, eng["w2"][0])
-        e1 = e1 + node_half("w1", 1)
-        pre = [forget(0, h3[0], e3[0], after=("w1", 1))]
         prepare("w2", 1, eng["w2"][1])
+        h3.append(child("v3", 2))
+        e3 = e3 + node_half("w3", 1)
+        h3.append(child("v3", 3))
+        gather_turn("v2", pre_g, 3, h2[3])
+        e1 = node_half("w1", 0) + node_half("w1", 1)
+        pre = [forget(0, h3[0], e3[0])]
+        quantize("w2", 0)
         pre.append(forget(1, h3[1], e3[1]))
-        e2 = node_half("w2", 0)
-        pre.append(forget(2, h3[2], e3[2], after=("w2", 0)))
-        e2 = e2 + node_half("w2", 1)
-        pre.append(forget(3, h3[3], e3[3], after=("w2", 1)))
-        f = [squash(t, pre[t]) for t in range(PACK)]
+        quantize("w2", 1)
+        pre.append(forget(2, h3[2], e3[2]))
+        pre.append(forget(3, h3[3], e3[3]))
+        f = [squash(0, pre[0])]
         a = close("a", pre_a, e1, ACT.Sigmoid)
+        f.append(squash(1, pre[1]))
+        e2 = node_half("w2", 0) + node_half("w2", 1)
+        f = f + [squash(t, pre[t]) for t in (2, 3)]
         g = close("g", pre_g, e2, ACT.Tanh)
 
         fc0 = sb("fc0", [P, PACK, V], F32)

@@ -26,7 +26,7 @@ def tile_picked_ztree_cell_po_kernel(
     nc = tc.nc
     with ExitStack() as ctx:
         keep = ctx.enter_context(tc.tile_pool(name="keep", bufs=1))
-        mm = ctx.enter_context(tc.psum_pool(name="mm", bufs=2))
+        mm = ctx.enter_context(tc.psum_pool(name="mm", bufs=4))
         held = ctx.enter_context(tc.psum_pool(name="held", bufs=1))
 
         def sb(name, shape, dtype, tag=None):
@@ -52,6 +52,7 @@ def tile_picked_ztree_cell_po_kernel(
         def load(name, src, c0, c1):
             raw = sb("raw_%s_%d" % (name, c0), [P, PACK, c1 - c0], F32)
             nc.sync.dma_start(out=raw[:], in_=src.rearrange("(p j) c -> p j c", j=PACK)[:, :, c0:c1])
+            raws[(name, None)] = raw[:]
             for c in range(c0, c1, HALF):
                 raws[(name, c // HALF)] = raw[:, :, c - c0 : c - c0 + HALF]
 
@@ -63,26 +64,19 @@ def tile_picked_ztree_cell_po_kernel(
             )
         load("v1", v1, 0, HALF)
         load("v1", v1, HALF, N)
+        load("v2", v2, 0, HALF)
         nc.sync.dma_start(pos_sb[0][:], pos1)
         nc.sync.dma_start(pos_sb[1][:], pos2)
-        load("v2", v2, 0, HALF)
         load("v2", v2, HALF, N)
+        load("v3", v3, 0, N)
         load("eT", eT, 0, V)
-        for name, src in (("w1", w1), ("v3", v3), ("w3", w3), ("w2", w2)):
+        for name, src in (("w3", w3), ("w1", w1), ("w2", w2)):
             load(name, src, 0, N)
         for t in range(PACK):
             nc.sync.dma_start(out=cell_sb[t][:], in_=cell_rows[:, t, :])
 
-        slot = {
-            ("v2", 0): "bf_v1_1",
-            ("w1", 0): "h_v1_0",
-            ("w1", 1): "h_v1_1",
-            ("v3", 0): "h_v1_2",
-            ("w3", 0): "h_v2_0",
-            ("w2", 0): "u_v2_1",
-            ("w2", 1): "u_v2_2",
-        }
-        window_slot = {("v2", 2): "raw_v3_0", ("v2", 3): "raw_w3_0"}
+        slot = {}
+        window_slot = {}
         staged = {}
         codes = {}
 
@@ -95,40 +89,25 @@ def tile_picked_ztree_cell_po_kernel(
                 nc.scalar.copy(out=dst, in_=src)
 
         def prepare(name, half, engine):
+            c0, c1 = (0, N) if half is None else (HALF * half, HALF * half + HALF)
             raw = raws[(name, half)]
-            pieces = 2 if engine == "g" else 1
-            width = HALF // pieces
+            bf = sb("bf_%s_%s" % (name, half), [P, c1 - c0, PACK], BF16, tag=slot.get((name, half)))
+            staged[(name, half)] = bf[:].rearrange("p c j -> p (c j)")
             if name in ("v3", "w3"):
-                if (name, 0) not in staged:
-                    both = sb("bf_" + name, [P, PACK, P, PACK], BF16, tag=slot.get((name, 0)))
-                    for u in range(2):
-                        staged[(name, u)] = both[:, 2 * u : 2 * u + 2, :, :].rearrange("p t m j -> p (t m j)")
-                    staged[name] = both
-                for c in range(0, HALF, width):
-                    m0 = (HALF * half + c) // PACK
-                    cast(
-                        engine,
-                        staged[name][:, :, m0 : m0 + width // PACK, :].rearrange("p t m j -> p m j t"),
-                        raw[:, :, c : c + width].rearrange("p j (m t) -> p m j t", t=PACK),
-                    )
+                cast(engine, bf[:].rearrange("p (t m) j -> p m j t", t=PACK), raw.rearrange("p j (m t) -> p m j t", t=PACK))
             else:
-                bf = sb("bf_%s_%d" % (name, half), [P, HALF, PACK], BF16, tag=slot.get((name, half)))
-                staged[(name, half)] = bf[:].rearrange("p c j -> p (c j)")
-                for c in range(0, HALF, width):
-                    if engine == "g":
-                        cast(engine, bf[:, c : c + width, :], raw[:, :, c : c + width].rearrange("p j c -> p c j"))
-                    else:
-                        cast(
-                            engine,
-                            bf[:].rearrange("p (c i) j -> p c j i", i=4),
-                            raw.rearrange("p j (c i) -> p c j i", i=4),
-                        )
+                cast(engine, bf[:].rearrange("p (c i) j -> p c j i", i=4), raw.rearrange("p j (c i) -> p c j i", i=4))
 
         def quantize(name, half):
-            cw = sb("cw_%s_%d" % (name, half), [P, HALF], U32)
-            cs = sb("cs_%s_%d" % (name, half), [P, HALF], U8)
+            width = N if half is None else HALF
+            cw = sb("cw_%s_%s" % (name, half), [P, width], U32)
+            cs = sb("cs_%s_%s" % (name, half), [P, width], U8)
             nc.vector.quantize_mx(out=cw[:].bitcast(FP8X4), scales=cs[:], in_=staged[(name, half)])
-            codes[(name, half)] = (cw, cs)
+            for u in range(2):
+                if half is None:
+                    codes[(name, u)] = (cw[:, HALF * u : HALF * u + HALF], cs[:, HALF * u : HALF * u + HALF])
+                elif half == u:
+                    codes[(name, u)] = (cw[:], cs[:])
 
         xw = sb("xw", [P, S], U32)
         xs = sb("xs", [P, S], U8)
@@ -153,11 +132,16 @@ def tile_picked_ztree_cell_po_kernel(
             nc.scalar.copy(out=h[:], in_=acc[:])
             return h
 
-        def node_half(name, half):
+        def node_product(name, half):
             acc = mm.tile([P, S], F32, name="acc")
             ew, es = codes[("eT", 0)]
             for u in range(2):
-                product(acc[:, V * u : V * u + V], name, 2 * half + u, ew[:], es[:])
+                product(acc[:, V * u : V * u + V], name, 2 * half + u, ew, es)
+            return acc
+
+        def node_half(name, half, acc=None):
+            if acc is None:
+                acc = node_product(name, half)
             e = sb("e_%s_%d" % (name, half), [P, 2, V], F32)
             nc.scalar.copy(out=e[:].rearrange("p u v -> p (u v)"), in_=acc[:])
             return [e[:, 0, :], e[:, 1, :]]
@@ -190,84 +174,95 @@ def tile_picked_ztree_cell_po_kernel(
                 res.append(gate)
             return res
 
-        def forget(t, window, e, after=None):
-            pre = sb("pre_f%d" % t, [P, 2, V], F32, tag=tag_of(after))
-            for d in range(2):
-                nc.vector.tensor_tensor(pre[:, d, :], window[:].indirect(pos_sb[d][:]), e, ALU.add)
-            return pre
+        pre_f = {0: sb("pre_f0", [P, PACK, V], F32)}
+        f0 = sb("f0", [P, PACK, V], F32)
+        f1 = {}
 
-        def squash(t, pre):
-            f = sb("f%d" % t, [P, 2, V], F32)
-            nc.scalar.activation(f[:].rearrange("p d v -> p (d v)"), pre[:].rearrange("p d v -> p (d v)"), ACT.Sigmoid)
-            return f
+        def forget(d, t):
+            nc.vector.tensor_tensor(pre_f[d][:, t, :], h3[t][:].indirect(pos_sb[d][:]), e3[t], ALU.add)
+
+        def squash_first(u):
+            nc.scalar.activation(f0[:, 2 * u : 2 * u + 2, :], pre_f[0][:, 2 * u : 2 * u + 2, :], ACT.Sigmoid)
+
+        def squash_second(hv):
+            f1[hv] = sb("f1_%d" % hv, [P, PACK, P], F32, tag=("cw_w2_None", "cs_w2_None")[hv])
+            nc.scalar.activation(f1[hv][:], pre_f[1][:, :, P * hv : P * hv + P], ACT.Sigmoid)
 
         pre_a = [held.tile([P, N], F32, name="pre_a%d" % hv) for hv in range(2)]
         pre_g = [held.tile([P, N], F32, name="pre_g%d" % hv) for hv in range(2)]
-        total = [held.tile([P, N], F32, name="total%d" % hv) for hv in range(2)]
-        eng = {"v1": "sv", "v2": "vg", "v3": "ss", "eT": "g", "w3": "ss", "w1": "gg", "w2": "gg"}
+        eng = {"v1": "ss", "v2": "vs", "v3": "ss", "eT": "v", "w3": "ss", "w1": "vs", "w2": "ss"}
 
         nc.vector.tensor_copy(xw[:], xw_all[:].bitcast(U32).indirect(offs_sb[:]))
         nc.vector.tensor_copy(xs[:], xs_all[:].indirect(offs_sb[:]))
+        h1, h2, h3 = {}, {}, {}
+        e1, e2, e3 = [], [], []
         prepare("v1", 0, eng["v1"][0])
         quantize("v1", 0)
-        h1 = [child("v1", 0), child("v1", 1)]
+        h1[0] = child("v1", 0)
+        h1[1] = child("v1", 1)
         prepare("v1", 1, eng["v1"][1])
         quantize("v1", 1)
         prepare("v2", 0, eng["v2"][0])
         prepare("v2", 1, eng["v2"][1])
         gather_turn("v1", pre_a, 0, h1[0])
         quantize("v2", 0)
-        h1 = h1 + [child("v1", 2), child("v1", 3)]
+        h1[2] = child("v1", 2)
+        h1[3] = child("v1", 3)
         gather_turn("v1", pre_a, 1, h1[1])
         quantize("v2", 1)
+        prepare("v3", None, "s")
         prepare("eT", 0, eng["eT"][0])
-        h2 = [child("v2", 0)]
+        h2[0] = child("v2", 0)
+        h2[1] = child("v2", 1)
         gather_turn("v1", pre_a, 2, h1[2])
-        prepare("w1", 0, eng["w1"][0])
-        h2.append(child("v2", 1))
         gather_turn("v1", pre_a, 3, h1[3])
-        quantize("eT", 0)
-        prepare("w1", 1, eng["w1"][1])
-        prepare("v3", 0, eng["v3"][0])
-        prepare("v3", 1, eng["v3"][1])
-        h2.append(child("v2", 2))
+        quantize("v3", None)
+        prepare("w3", None, "s")
         gather_turn("v2", pre_g, 0, h2[0])
+        quantize("eT", 0)
+        gather_turn("v2", pre_g, 1, h2[1])
+        prepare("w1", 0, eng["w1"][0])
+        quantize("w3", None)
+        h2[2] = child("v2", 2)
+        h2[3] = child("v2", 3)
+        prepare("w1", 1, eng["w1"][1])
+        early = [node_product("w3", half) for half in range(2)]
+        h3[0] = child("v3", 0)
+        h3[1] = child("v3", 1)
+        e3.extend(node_half("w3", 0, early[0]))
+        prepare("w2", None, "s")
+        h3[2] = child("v3", 2)
+        e3.extend(node_half("w3", 1, early[1]))
+        h3[3] = child("v3", 3)
+        gather_turn("v2", pre_g, 2, h2[2])
+        gather_turn("v2", pre_g, 3, h2[3])
         quantize("w1", 0)
         quantize("w1", 1)
-        gather_turn("v2", pre_g, 1, h2[1])
-        prepare("w3", 0, eng["w3"][0])
-        quantize("v3", 0)
-        quantize("v3", 1)
-        prepare("w3", 1, eng["w3"][1])
-        h2.append(child("v2", 3))
-        h3 = [child("v3", 0), child("v3", 1)]
-        gather_turn("v2", pre_g, 2, h2[2])
-        quantize("w3", 0)
-        quantize("w3", 1)
-        e3 = node_half("w3", 0)
-        prepare("w2", 0, eng["w2"][0])
-        prepare("w2", 1, eng["w2"][1])
-        h3.append(child("v3", 2))
-        e3 = e3 + node_half("w3", 1)
-        h3.append(child("v3", 3))
-        gather_turn("v2", pre_g, 3, h2[3])
-        e1 = node_half("w1", 0) + node_half("w1", 1)
-        pre = [forget(0, h3[0], e3[0])]
-        quantize("w2", 0)
-        pre.append(forget(1, h3[1], e3[1]))
-        quantize("w2", 1)
-        pre.append(forget(2, h3[2], e3[2]))
-        pre.append(forget(3, h3[3], e3[3]))
-        f = [squash(0, pre[0])]
+        forget(0, 0)
+        forget(0, 1)
+        quantize("w2", None)
+        forget(0, 2)
+        forget(0, 3)
+        e1.extend(node_half("w1", 0))
+        e1.extend(node_half("w1", 1))
+        e2.extend(node_half("w2", 0))
+        e2.extend(node_half("w2", 1))
+        pre_f[1] = sb("pre_f1", [P, PACK, V], F32, tag="raw_w2_0")
+        forget(1, 0)
+        forget(1, 1)
+        forget(1, 2)
+        forget(1, 3)
+        squash_first(0)
+        squash_first(1)
         a = close("a", pre_a, e1, ACT.Sigmoid)
-        f.append(squash(1, pre[1]))
-        e2 = node_half("w2", 0) + node_half("w2", 1)
-        f = f + [squash(t, pre[t]) for t in (2, 3)]
         g = close("g", pre_g, e2, ACT.Tanh)
+        squash_second(0)
+        squash_second(1)
 
+        total = [mm.tile([P, N], F32, name="total%d" % hv, tag="acc") for hv in range(2)]
         fc0 = sb("fc0", [P, PACK, V], F32)
         for t in range(PACK):
-            nc.vector.tensor_tensor(fc0[:, t, :], cell_sb[t][:].indirect(pos_sb[0][:]), f[t][:, 0, :], ALU.mult)
+            nc.vector.tensor_tensor(fc0[:, t, :], cell_sb[t][:].indirect(pos_sb[0][:]), f0[:, t, :], ALU.mult)
         for hv in range(2):
             ag = sb("ag%d" % hv, [P, N], F32)
             nc.vector.tensor_tensor(ag[:], a[hv][:], g[hv][:], ALU.mult)
@@ -293,7 +288,7 @@ def tile_picked_ztree_cell_po_kernel(
                 nc.vector.tensor_tensor(
                     piece[:, t, :],
                     cell_sb[t][:].indirect(pos_sb[1][:, 8 * hv : 8 * hv + 8]),
-                    f[t][:, 1, P * hv : P * hv + P],
+                    f1[hv][:, t, :],
                     ALU.mult,
                 )
             fc1.append(piece)

@@ -16,7 +16,9 @@ ALU = mybir.AluOpType
 K, T, S, V, N = 512, 1024, 512, 256, 512
 P = 128
 PACK = 4
-HALF = 256
+QUADRANTS = 4
+HALF = N // 2
+LINE = 4
 FLOPS = 2 * K * N * 3 * (S + V)
 
 
@@ -26,11 +28,10 @@ def tile_picked_ztree_cell_po_kernel(
     nc = tc.nc
     with ExitStack() as ctx:
         keep = ctx.enter_context(tc.tile_pool(name="keep", bufs=1))
-        mm = ctx.enter_context(tc.psum_pool(name="mm", bufs=4))
         held = ctx.enter_context(tc.psum_pool(name="held", bufs=1))
 
-        def sb(name, shape, dtype, tag=None):
-            return keep.tile(shape, dtype, name=name, tag=tag or name, align_bytes=64)
+        def sb(name, shape, dtype, place=None):
+            return keep.tile(shape, dtype, name=name, tag=place or name, align_bytes=64)
 
         offs_sb = keep.tile([P, S // 16], U16, name="offs_sb")
         pos_sb = [keep.tile([P, V // 16], U16, name="pos_sb%d" % d) for d in range(2)]
@@ -43,22 +44,17 @@ def tile_picked_ztree_cell_po_kernel(
         ident = sb("ident", [P, P], F32)
         make_identity(nc, ident[:])
 
-        cell_sb = [sb("cell%d" % t, [P, S], F32) for t in range(PACK)]
-        cell_rows = cell.rearrange("(p t) s -> p t s", t=PACK)
-        xw_all = sb("xw_all", [P, T], I32)
-
         raws = {}
 
         def load(name, src, c0, c1):
             raw = sb("raw_%s_%d" % (name, c0), [P, PACK, c1 - c0], F32)
             nc.sync.dma_start(out=raw[:], in_=src.rearrange("(p j) c -> p j c", j=PACK)[:, :, c0:c1])
-            raws[(name, None)] = raw[:]
-            for c in range(c0, c1, HALF):
-                raws[(name, c // HALF)] = raw[:, :, c - c0 : c - c0 + HALF]
+            raws[name] = raws.get(name, []) + [(c0, c1, raw)]
 
+        xw_all = sb("xw_all", [P, T], I32)
         nc.sync.dma_start(offs_sb[:], offs)
         nc.sync.dma_start(out=xw_all[:], in_=x_words[0].rearrange("p c r -> p (c r)").bitcast(I32))
-        for q in range(4):
+        for q in range(QUADRANTS):
             nc.sync.dma_start(
                 out=xs_all[32 * q : 32 * q + 4, :].bitcast(I32), in_=x_scales[0, 4 * q : 4 * q + 4, :].bitcast(I32)
             )
@@ -70,247 +66,217 @@ def tile_picked_ztree_cell_po_kernel(
         load("v2", v2, HALF, N)
         load("v3", v3, 0, N)
         load("eT", eT, 0, V)
-        for name, src in (("w3", w3), ("w1", w1), ("w2", w2)):
-            load(name, src, 0, N)
+        load("w3", w3, 0, N)
+        load("w1", w1, 0, N)
+        load("w2", w2, 0, N)
+        cell_sb = [sb("cell%d" % t, [P, S], F32) for t in range(PACK)]
         for t in range(PACK):
-            nc.sync.dma_start(out=cell_sb[t][:], in_=cell_rows[:, t, :])
+            nc.sync.dma_start(out=cell_sb[t][:], in_=cell.rearrange("(p t) s -> p t s", t=PACK)[:, t, :])
 
-        slot = {}
-        window_slot = {}
+        on_scalar, on_vector = nc.scalar.copy, nc.vector.tensor_copy
         staged = {}
         codes = {}
 
-        def cast(engine, dst, src):
-            if engine == "g":
-                nc.gpsimd.tensor_scalar(dst, src, 1.0, 0.0, ALU.mult, ALU.add)
-            elif engine == "v":
-                nc.vector.tensor_copy(out=dst, in_=src)
+        def interleave(copy, dst, src):
+            copy(out=dst.rearrange("p (c i) j -> p c j i", i=LINE), in_=src.rearrange("p j (c i) -> p c j i", i=LINE))
+
+        def stage(copy, name, c0, c1, deal=False):
+            a0, raw = [(a0, raw) for a0, a1, raw in raws[name] if a0 <= c0 < a1][0]
+            src = raw[:, :, c0 - a0 : c1 - a0]
+            bf = sb("bf_%s_%d" % (name, c0), [P, c1 - c0, PACK], BF16)
+            if deal:
+                copy(out=bf[:].rearrange("p (t m) j -> p m j t", t=PACK), in_=src.rearrange("p j (m t) -> p m j t", t=PACK))
             else:
-                nc.scalar.copy(out=dst, in_=src)
+                interleave(copy, bf[:], src)
+            staged[(name, c0)] = bf
 
-        def prepare(name, half, engine):
-            c0, c1 = (0, N) if half is None else (HALF * half, HALF * half + HALF)
-            raw = raws[(name, half)]
-            bf = sb("bf_%s_%s" % (name, half), [P, c1 - c0, PACK], BF16, tag=slot.get((name, half)))
-            staged[(name, half)] = bf[:].rearrange("p c j -> p (c j)")
-            if name in ("v3", "w3"):
-                cast(engine, bf[:].rearrange("p (t m) j -> p m j t", t=PACK), raw.rearrange("p j (m t) -> p m j t", t=PACK))
-            else:
-                cast(engine, bf[:].rearrange("p (c i) j -> p c j i", i=4), raw.rearrange("p j (c i) -> p c j i", i=4))
+        def quantize(name, c0, c1):
+            words = sb("words_%s_%d" % (name, c0), [P, c1 - c0], U32)
+            scales = sb("scales_%s_%d" % (name, c0), [P, c1 - c0], U8)
+            nc.vector.quantize_mx(
+                out=words[:].bitcast(FP8X4), scales=scales[:], in_=staged[(name, c0)][:].rearrange("p c j -> p (c j)")
+            )
+            for c in range(c0, c1, P):
+                codes[(name, c // P)] = (words[:, c - c0 : c - c0 + P], scales[:, c - c0 : c - c0 + P])
+            return words, scales
 
-        def quantize(name, half):
-            width = N if half is None else HALF
-            cw = sb("cw_%s_%s" % (name, half), [P, width], U32)
-            cs = sb("cs_%s_%s" % (name, half), [P, width], U8)
-            nc.vector.quantize_mx(out=cw[:].bitcast(FP8X4), scales=cs[:], in_=staged[(name, half)])
-            for u in range(2):
-                if half is None:
-                    codes[(name, u)] = (cw[:, HALF * u : HALF * u + HALF], cs[:, HALF * u : HALF * u + HALF])
-                elif half == u:
-                    codes[(name, u)] = (cw[:], cs[:])
-
-        xw = sb("xw", [P, S], U32)
-        xs = sb("xs", [P, S], U8)
-
-        def product(out, name, i, moving, moving_scale):
-            cw, cs = codes[(name, i // 2)]
-            cols = slice(P * (i % 2), P * (i % 2) + P)
+        def product(out, name, i, moving):
+            words, scales = codes[(name, i)]
             nc.tensor.matmul_mx(
                 out=out,
-                lhsT=cw[:, cols].bitcast(FP8X4),
-                lhsT_scale=cs[:, cols],
-                rhs=moving.bitcast(FP8X4),
-                rhs_scale=moving_scale,
+                lhsT=words.bitcast(FP8X4),
+                lhsT_scale=scales,
+                rhs=moving[0][:].bitcast(FP8X4),
+                rhs_scale=moving[1][:],
                 start=True,
                 stop=True,
             )
 
-        def child(name, i):
-            acc = mm.tile([P, S], F32, name="acc")
-            product(acc[:], name, i, xw[:], xs[:])
-            h = sb("h_%s_%d" % (name, i), [P, S], F32, tag=window_slot.get((name, i)))
-            nc.scalar.copy(out=h[:], in_=acc[:])
+        def child_rows(name, i, h):
+            bank = held.tile([P, S], F32, name="bank%d" % (2 + i % 2 if name == "v3" else i))
+            product(bank[:], name, i, x_picked)
+            nc.scalar.copy(out=h, in_=bank[:])
             return h
 
-        def node_product(name, half):
-            acc = mm.tile([P, S], F32, name="acc")
-            ew, es = codes[("eT", 0)]
-            for u in range(2):
-                product(acc[:, V * u : V * u + V], name, 2 * half + u, ew, es)
-            return acc
+        def child_pair(name, i, place=None):
+            pair = sb("h_%s_%d" % (name, i), [P, 2, S], F32, place)
+            return [child_rows(name, i + u, pair[:, u, :]) for u in range(2)]
 
-        def node_half(name, half, acc=None):
-            if acc is None:
-                acc = node_product(name, half)
-            e = sb("e_%s_%d" % (name, half), [P, 2, V], F32)
-            nc.scalar.copy(out=e[:].rearrange("p u v -> p (u v)"), in_=acc[:])
+        def child_block(i, place=None):
+            return child_rows("v3", i, sb("h_v3_%d" % i, [P, S], F32, place)[:])
+
+        def node_pair(name, i):
+            bank = held.tile([P, 2 * V], F32, name="bank%d" % (i // 2))
+            for u in range(2):
+                product(bank[:, V * u : V * u + V], name, i + u, e_codes)
+            return bank
+
+        def node_rows(name, i, bank):
+            e = sb("e_%s_%d" % (name, i), [P, 2, V], F32)
+            nc.scalar.copy(out=e[:].rearrange("p u v -> p (u v)"), in_=bank[:])
             return [e[:, 0, :], e[:, 1, :]]
 
         def turn(bank, i, block, start, stop):
             nc.tensor.matmul(bank[:, P * i : P * i + P], block, ident[:], start=start, stop=stop, is_transpose=True)
 
-        def tag_of(after):
-            return after and (slot.get(after) or "bf_%s_%d" % after)
-
-        def gather_turn(name, banks, i, window, after=None):
-            got = sb("u_%s_%d" % (name, i), [P, 2, V], F32, tag=tag_of(after))
+        def gather_children(name, banks, i, h):
+            picked = sb("picked_%s_%d" % (name, i), [P, 2, V], F32)
             for d in range(2):
-                nc.vector.tensor_copy(got[:, d, :], window[:].indirect(pos_sb[d][:]))
+                nc.vector.tensor_copy(picked[:, d, :], h.indirect(pos_sb[d][:]))
             for d in range(2):
-                for hv in range(2):
-                    turn(banks[hv], i, got[:, d, P * hv : P * hv + P], i == 0 and d == 0, False)
+                for half in range(2):
+                    turn(banks[half], i, picked[:, d, P * half : P * half + P], i == 0 and d == 0, False)
 
-        def close(name, banks, e, func):
-            res = []
-            for hv in range(2):
+        def close_gate(name, banks, e, func):
+            gates = []
+            for half in range(2):
                 for i in range(PACK):
-                    turn(banks[hv], i, e[i][:, P * hv : P * hv + P], False, i == PACK - 1)
-                gate = sb("%s%d" % (name, hv), [P, N], F32)
+                    turn(banks[half], i, e[i][:, P * half : P * half + P], False, i == PACK - 1)
+                gate = sb("%s%d" % (name, half), [P, N], F32)
                 nc.scalar.activation(
-                    gate[:].rearrange("v (t p) -> v p t", t=PACK),
-                    banks[hv][:].rearrange("v (p t) -> v p t", t=PACK),
-                    func,
+                    gate[:].rearrange("v (t p) -> v p t", t=PACK), banks[half][:].rearrange("v (p t) -> v p t", t=PACK), func
                 )
-                res.append(gate)
-            return res
+                gates.append(gate)
+            return gates
 
-        pre_f = {0: sb("pre_f0", [P, PACK, V], F32)}
-        f0 = sb("f0", [P, PACK, V], F32)
-        f1 = {}
+        def gather_forget(pre, d, t):
+            nc.vector.tensor_tensor(pre[:, t, :], h3[t].indirect(pos_sb[d][:]), e3[t], ALU.add)
 
-        def forget(d, t):
-            nc.vector.tensor_tensor(pre_f[d][:, t, :], h3[t][:].indirect(pos_sb[d][:]), e3[t], ALU.add)
+        def forget_gate(f, pre):
+            for t in range(0, PACK, 2):
+                nc.scalar.activation(f[:, t : t + 2, :], pre[:, t : t + 2, :], ACT.Sigmoid)
 
-        def squash_first(u):
-            nc.scalar.activation(f0[:, 2 * u : 2 * u + 2, :], pre_f[0][:, 2 * u : 2 * u + 2, :], ACT.Sigmoid)
+        def gather_cells(name, f, d, v0, width):
+            fc = sb(name, [P, PACK, width], F32)
+            picks = pos_sb[d][:, v0 // 16 : (v0 + width) // 16]
+            for t in range(PACK):
+                nc.vector.tensor_tensor(fc[:, t, :], cell_sb[t][:].indirect(picks), f[:, t, v0 : v0 + width], ALU.mult)
+            return fc
 
-        def squash_second(hv):
-            f1[hv] = sb("f1_%d" % hv, [P, PACK, P], F32, tag=("cw_w2_None", "cs_w2_None")[hv])
-            nc.scalar.activation(f1[hv][:], pre_f[1][:, :, P * hv : P * hv + P], ACT.Sigmoid)
+        sum_a = [held.tile([P, N], F32, name="sum_a%d" % half) for half in range(2)]
+        sum_g = [held.tile([P, N], F32, name="sum_g%d" % half) for half in range(2)]
 
-        pre_a = [held.tile([P, N], F32, name="pre_a%d" % hv) for hv in range(2)]
-        pre_g = [held.tile([P, N], F32, name="pre_g%d" % hv) for hv in range(2)]
-        eng = {"v1": "ss", "v2": "vs", "v3": "ss", "eT": "v", "w3": "ss", "w1": "vs", "w2": "ss"}
+        x_picked = (sb("xw", [P, S], U32), sb("xs", [P, S], U8))
+        nc.vector.tensor_copy(x_picked[0][:], xw_all[:].bitcast(U32).indirect(offs_sb[:]))
+        nc.vector.tensor_copy(x_picked[1][:], xs_all[:].indirect(offs_sb[:]))
 
-        nc.vector.tensor_copy(xw[:], xw_all[:].bitcast(U32).indirect(offs_sb[:]))
-        nc.vector.tensor_copy(xs[:], xs_all[:].indirect(offs_sb[:]))
-        h1, h2, h3 = {}, {}, {}
-        e1, e2, e3 = [], [], []
-        prepare("v1", 0, eng["v1"][0])
-        quantize("v1", 0)
-        h1[0] = child("v1", 0)
-        h1[1] = child("v1", 1)
-        prepare("v1", 1, eng["v1"][1])
-        quantize("v1", 1)
-        prepare("v2", 0, eng["v2"][0])
-        prepare("v2", 1, eng["v2"][1])
-        gather_turn("v1", pre_a, 0, h1[0])
-        quantize("v2", 0)
-        h1[2] = child("v1", 2)
-        h1[3] = child("v1", 3)
-        gather_turn("v1", pre_a, 1, h1[1])
-        quantize("v2", 1)
-        prepare("v3", None, "s")
-        prepare("eT", 0, eng["eT"][0])
-        h2[0] = child("v2", 0)
-        h2[1] = child("v2", 1)
-        gather_turn("v1", pre_a, 2, h1[2])
-        gather_turn("v1", pre_a, 3, h1[3])
-        quantize("v3", None)
-        prepare("w3", None, "s")
-        gather_turn("v2", pre_g, 0, h2[0])
-        quantize("eT", 0)
-        gather_turn("v2", pre_g, 1, h2[1])
-        prepare("w1", 0, eng["w1"][0])
-        quantize("w3", None)
-        h2[2] = child("v2", 2)
-        h2[3] = child("v2", 3)
-        prepare("w1", 1, eng["w1"][1])
-        early = [node_product("w3", half) for half in range(2)]
-        h3[0] = child("v3", 0)
-        h3[1] = child("v3", 1)
-        e3.extend(node_half("w3", 0, early[0]))
-        prepare("w2", None, "s")
-        h3[2] = child("v3", 2)
-        e3.extend(node_half("w3", 1, early[1]))
-        h3[3] = child("v3", 3)
-        gather_turn("v2", pre_g, 2, h2[2])
-        gather_turn("v2", pre_g, 3, h2[3])
-        quantize("w1", 0)
-        quantize("w1", 1)
-        forget(0, 0)
-        forget(0, 1)
-        quantize("w2", None)
-        forget(0, 2)
-        forget(0, 3)
-        e1.extend(node_half("w1", 0))
-        e1.extend(node_half("w1", 1))
-        e2.extend(node_half("w2", 0))
-        e2.extend(node_half("w2", 1))
-        pre_f[1] = sb("pre_f1", [P, PACK, V], F32, tag="raw_w2_0")
-        forget(1, 0)
-        forget(1, 1)
-        forget(1, 2)
-        forget(1, 3)
-        squash_first(0)
-        squash_first(1)
-        a = close("a", pre_a, e1, ACT.Sigmoid)
-        g = close("g", pre_g, e2, ACT.Tanh)
-        squash_second(0)
-        squash_second(1)
+        for i in range(2):
+            stage(on_scalar, "v1", P * i, P * i + P)
+            quantize("v1", P * i, P * i + P)
+        h1 = child_pair("v1", 0)
+        stage(on_vector, "v1", HALF, N)
+        quantize("v1", HALF, N)
+        stage(on_vector, "v2", 0, HALF)
+        stage(on_scalar, "v2", HALF, N)
+        gather_children("a", sum_a, 0, h1[0])
+        quantize("v2", 0, HALF)
+        h1 = h1 + child_pair("v1", 2, "raw_v2_%d" % HALF)
+        gather_children("a", sum_a, 1, h1[1])
+        quantize("v2", HALF, N)
+        stage(on_scalar, "v3", 0, N, deal=True)
+        stage(on_vector, "eT", 0, V)
+        h2 = child_pair("v2", 0, "raw_v3_0")
+        gather_children("a", sum_a, 2, h1[2])
+        gather_children("a", sum_a, 3, h1[3])
 
-        total = [mm.tile([P, N], F32, name="total%d" % hv, tag="acc") for hv in range(2)]
-        fc0 = sb("fc0", [P, PACK, V], F32)
+        quantize("v3", 0, N)
+        stage(on_scalar, "w3", 0, N, deal=True)
+        gather_children("g", sum_g, 0, h2[0])
+        e_codes = quantize("eT", 0, V)
+        gather_children("g", sum_g, 1, h2[1])
+        stage(on_vector, "w1", 0, N)
+        quantize("w3", 0, N)
+        h2 = h2 + child_pair("v2", 2, "raw_w3_0")
+        e3_banks = [node_pair("w3", i) for i in (0, 2)]
+        h3 = [child_block(0), child_block(1)]
+        e3 = node_rows("w3", 0, e3_banks[0])
+        stage(on_scalar, "w2", 0, N)
+        h3.append(child_block(2))
+        e3 = e3 + node_rows("w3", 2, e3_banks[1])
+        h3.append(child_block(3))
+        gather_children("g", sum_g, 2, h2[2])
+        gather_children("g", sum_g, 3, h2[3])
+        quantize("w1", 0, N)
+
+        pre_first = sb("pre_first", [P, PACK, V], F32)
+        gather_forget(pre_first, 0, 0)
+        gather_forget(pre_first, 0, 1)
+        quantize("w2", 0, N)
+        gather_forget(pre_first, 0, 2)
+        gather_forget(pre_first, 0, 3)
+        e1, e2 = [], []
+        for name, e in (("w1", e1), ("w2", e2)):
+            for i in (0, 2):
+                e.extend(node_rows(name, i, node_pair(name, i)))
+        pre_second = sb("pre_second", [P, PACK, V], F32, "raw_w2_0")
         for t in range(PACK):
-            nc.vector.tensor_tensor(fc0[:, t, :], cell_sb[t][:].indirect(pos_sb[0][:]), f0[:, t, :], ALU.mult)
-        for hv in range(2):
-            ag = sb("ag%d" % hv, [P, N], F32)
-            nc.vector.tensor_tensor(ag[:], a[hv][:], g[hv][:], ALU.mult)
-            for t in range(PACK):
-                turn(total[hv], t, ag[:, P * t : P * t + P], t == 0, False)
-        for hv in range(2):
-            bank = held.tile([P, N], F32, name="turned_fc%d" % hv, tag="pre_a%d" % hv)
-            for t in range(PACK):
-                turn(bank, t, fc0[:, t, P * hv : P * hv + P], True, True)
-            turned = sb("turned%d" % hv, [P, N], F32)
-            nc.scalar.copy(out=turned[:], in_=bank[:])
-            for t in range(PACK):
-                turn(total[hv], t, turned[:, P * t : P * t + P], False, t == PACK - 1)
+            gather_forget(pre_second, 1, t)
+        f_first = sb("f_first", [P, PACK, V], F32)
+        forget_gate(f_first, pre_first)
+        a = close_gate("a", sum_a, e1, ACT.Sigmoid)
+        g = close_gate("g", sum_g, e2, ACT.Tanh)
+        f_second = sb("f_second", [P, PACK, V], F32, "words_w2_0")
+        forget_gate(f_second, pre_second)
 
-        y_codes = sb("y_codes", [P, V], U32)
-        y_scales = sb("y_scales", [P, V], U8)
-        out_rows = out_0.rearrange("(p t) v -> p t v", t=PACK)
-        out_words = out_1[0].rearrange("p c r -> p (c r)").bitcast(I32)
-        fc1 = []
-        for hv in range(2):
-            piece = sb("fc1_%d" % hv, [P, PACK, P], F32)
+        total = [held.tile([P, N], F32, name="total%d" % half, tag="bank%d" % (2 + half)) for half in range(2)]
+        fc_first = gather_cells("fc_first", f_first, 0, 0, V)
+        for half in range(2):
+            ag = sb("ag%d" % half, [P, N], F32)
+            nc.vector.tensor_tensor(ag[:], a[half][:], g[half][:], ALU.mult)
             for t in range(PACK):
-                nc.vector.tensor_tensor(
-                    piece[:, t, :],
-                    cell_sb[t][:].indirect(pos_sb[1][:, 8 * hv : 8 * hv + 8]),
-                    f1[hv][:, t, :],
-                    ALU.mult,
-                )
-            fc1.append(piece)
-        for hv in range(2):
-            cols = slice(P * hv, P * hv + P)
-            y = sb("y%d" % hv, [P, PACK, P], F32)
+                turn(total[half], t, ag[:, P * t : P * t + P], t == 0, False)
+        for half in range(2):
+            once = held.tile([P, N], F32, name="once%d" % half, tag="sum_a%d" % half)
+            for t in range(PACK):
+                turn(once, t, fc_first[:, t, P * half : P * half + P], True, True)
+            turned = sb("turned%d" % half, [P, N], F32)
+            nc.scalar.copy(out=turned[:], in_=once[:])
+            for t in range(PACK):
+                turn(total[half], t, turned[:, P * t : P * t + P], False, t == PACK - 1)
+        fc_second = [gather_cells("fc_second%d" % half, f_second, 1, P * half, P) for half in range(2)]
+
+        y_words = sb("y_words", [P, V], U32)
+        y_scales = sb("y_scales", [P, V], U8)
+        for half, copy in enumerate((on_scalar, on_vector)):
+            nodes = slice(P * half, P * half + P)
+            y = sb("y%d" % half, [P, PACK, P], F32)
             nc.vector.tensor_tensor(
-                y[:].rearrange("p t v -> p (t v)"), total[hv][:], fc1[hv][:].rearrange("p t v -> p (t v)"), ALU.add
+                y[:].rearrange("p t v -> p (t v)"),
+                total[half][:],
+                fc_second[half][:].rearrange("p t v -> p (t v)"),
+                ALU.add,
             )
-            nc.sync.dma_start(out=out_rows[:, :, cols], in_=y[:])
-            y_bf = sb("y_bf%d" % hv, [P, P, PACK], BF16)
-            cast(
-                "sv"[hv],
-                y_bf[:].rearrange("p (c i) t -> p c t i", i=4),
-                y[:].rearrange("p t (c i) -> p c t i", i=4),
-            )
+            nc.sync.dma_start(out=out_0.rearrange("(p t) v -> p t v", t=PACK)[:, :, nodes], in_=y[:])
+            y_bf = sb("y_bf%d" % half, [P, P, PACK], BF16)
+            interleave(copy, y_bf[:], y[:])
             nc.vector.quantize_mx(
-                out=y_codes[:, cols].bitcast(FP8X4), scales=y_scales[:, cols], in_=y_bf[:].rearrange("p v t -> p (v t)")
+                out=y_words[:, nodes].bitcast(FP8X4),
+                scales=y_scales[:, nodes],
+                in_=y_bf[:].rearrange("p v t -> p (v t)"),
             )
-            nc.sync.dma_start(out=out_words[:, cols], in_=y_codes[:, cols].bitcast(I32))
-        for q in range(4):
-            queue = nc.sync if q % 2 == 0 else nc.scalar
+        nc.sync.dma_start(out=out_1[0].rearrange("p c r -> p (c r)").bitcast(I32), in_=y_words[:].bitcast(I32))
+        for q in range(QUADRANTS):
+            queue = nc.scalar if q % 2 == 0 else nc.sync
             queue.dma_start(
                 out=out_2[0, 4 * q : 4 * q + 4, :].bitcast(I32), in_=y_scales[32 * q : 32 * q + 4, :].bitcast(I32)
             )

from contextlib import ExitStack

import concourse.mybir as mybir
from concourse.masks import make_identity

F32 = mybir.dt.float32
BF16 = mybir.dt.bfloat16
I32 = mybir.dt.int32
U32 = mybir.dt.uint32
U16 = mybir.dt.uint16
U8 = mybir.dt.uint8
FP8X4 = mybir.dt.float8_e4m3fn_x4
ACT = mybir.ActivationFunctionType
ALU = mybir.AluOpType

K, T, S, V, N = 512, 1024, 512, 256, 512
P = 128
PACK = 4
QUADRANTS = 4
HALF = N // 2
LINE = 4
FLOPS = 2 * K * N * 3 * (S + V)


def tile_picked_ztree_cell_po_kernel(
    tc, x_words, x_scales, eT, w1, w2, w3, v1, v2, v3, cell, offs, pos1, pos2, out_0, out_1, out_2
):
    nc = tc.nc
    with ExitStack() as ctx:
        keep = ctx.enter_context(tc.tile_pool(name="keep", bufs=1))
        held = ctx.enter_context(tc.psum_pool(name="held", bufs=1))

        def sb(name, shape, dtype, place=None):
            return keep.tile(shape, dtype, name=name, tag=place or name, align_bytes=64)

        offs_sb = keep.tile([P, S // 16], U16, name="offs_sb")
        pos_sb = [keep.tile([P, V // 16], U16, name="pos_sb%d" % d) for d in range(2)]

        xs_all = sb("xs_all", [P, T], U8)
        nc.gpsimd.memset(xs_all[:].bitcast(I32), 0)
        warm = sb("warm", [P, 16], F32)
        nc.gpsimd.memset(warm[:, 0:8], 0.0)
        nc.scalar.activation(warm[:, 8:16], warm[:, 0:8], ACT.Sigmoid)
        ident = sb("ident", [P, P], F32)
        make_identity(nc, ident[:])

        raws = {}

        def load(name, src, c0, c1):
            raw = sb("raw_%s_%d" % (name, c0), [P, PACK, c1 - c0], F32)
            nc.sync.dma_start(out=raw[:], in_=src.rearrange("(p j) c -> p j c", j=PACK)[:, :, c0:c1])
            raws[name] = raws.get(name, []) + [(c0, c1, raw)]

        xw_all = sb("xw_all", [P, T], I32)
        nc.sync.dma_start(offs_sb[:], offs)
        nc.sync.dma_start(out=xw_all[:], in_=x_words[0].rearrange("p c r -> p (c r)").bitcast(I32))
        for q in range(QUADRANTS):
            nc.sync.dma_start(
                out=xs_all[32 * q : 32 * q + 4, :].bitcast(I32), in_=x_scales[0, 4 * q : 4 * q + 4, :].bitcast(I32)
            )
        load("v1", v1, 0, HALF)
        load("v1", v1, HALF, N)
        load("v2", v2, 0, HALF)
        nc.sync.dma_start(pos_sb[0][:], pos1)
        nc.sync.dma_start(pos_sb[1][:], pos2)
        load("v2", v2, HALF, N)
        load("v3", v3, 0, N)
        load("eT", eT, 0, V)
        load("w3", w3, 0, N)
        load("w1", w1, 0, N)
        load("w2", w2, 0, N)
        cell_sb = [sb("cell%d" % t, [P, S], F32) for t in range(PACK)]
        for t in range(PACK):
            nc.sync.dma_start(out=cell_sb[t][:], in_=cell.rearrange("(p t) s -> p t s", t=PACK)[:, t, :])

        on_scalar, on_vector = nc.scalar.copy, nc.vector.tensor_copy
        staged = {}
        codes = {}

        def interleave(copy, dst, src):
            copy(out=dst.rearrange("p (c i) j -> p c j i", i=LINE), in_=src.rearrange("p j (c i) -> p c j i", i=LINE))

        def stage(copy, name, c0, c1, deal=False):
            a0, raw = [(a0, raw) for a0, a1, raw in raws[name] if a0 <= c0 < a1][0]
            src = raw[:, :, c0 - a0 : c1 - a0]
            bf = sb("bf_%s_%d" % (name, c0), [P, c1 - c0, PACK], BF16)
            if deal:
                copy(out=bf[:].rearrange("p (t m) j -> p m j t", t=PACK), in_=src.rearrange("p j (m t) -> p m j t", t=PACK))
            else:
                interleave(copy, bf[:], src)
            staged[(name, c0)] = bf

        def quantize(name, c0, c1):
            words = sb("words_%s_%d" % (name, c0), [P, c1 - c0], U32)
            scales = sb("scales_%s_%d" % (name, c0), [P, c1 - c0], U8)
            nc.vector.quantize_mx(
                out=words[:].bitcast(FP8X4), scales=scales[:], in_=staged[(name, c0)][:].rearrange("p c j -> p (c j)")
            )
            for c in range(c0, c1, P):
                codes[(name, c // P)] = (words[:, c - c0 : c - c0 + P], scales[:, c - c0 : c - c0 + P])
            return words, scales

        def product(out, name, i, moving):
            words, scales = codes[(name, i)]
            nc.tensor.matmul_mx(
                out=out,
                lhsT=words.bitcast(FP8X4),
                lhsT_scale=scales,
                rhs=moving[0][:].bitcast(FP8X4),
                rhs_scale=moving[1][:],
                start=True,
                stop=True,
            )

        def child_rows(name, i, h):
            bank = held.tile([P, S], F32, name="bank%d" % (2 + i % 2 if name == "v3" else i))
            product(bank[:], name, i, x_picked)
            nc.scalar.copy(out=h, in_=bank[:])
            return h

        def child_pair(name, i, place=None):
            pair = sb("h_%s_%d" % (name, i), [P, 2, S], F32, place)
            return [child_rows(name, i + u, pair[:, u, :]) for u in range(2)]

        def child_block(i, place=None):
            return child_rows("v3", i, sb("h_v3_%d" % i, [P, S], F32, place)[:])

        def node_pair(name, i):
            bank = held.tile([P, 2 * V], F32, name="bank%d" % (i // 2))
            for u in range(2):
                product(bank[:, V * u : V * u + V], name, i + u, e_codes)
            return bank

        def node_rows(name, i, bank):
            e = sb("e_%s_%d" % (name, i), [P, 2, V], F32)
            nc.scalar.copy(out=e[:].rearrange("p u v -> p (u v)"), in_=bank[:])
            return [e[:, 0, :], e[:, 1, :]]

        def turn(bank, i, block, start, stop):
            nc.tensor.matmul(bank[:, P * i : P * i + P], block, ident[:], start=start, stop=stop, is_transpose=True)

        def gather_children(name, banks, i, h):
            picked = sb("picked_%s_%d" % (name, i), [P, 2, V], F32)
            for d in range(2):
                nc.vector.tensor_copy(picked[:, d, :], h.indirect(pos_sb[d][:]))
            for d in range(2):
                for half in range(2):
                    turn(banks[half], i, picked[:, d, P * half : P * half + P], i == 0 and d == 0, False)

        def close_gate(name, banks, e, func):
            gates = []
            for half in range(2):
                for i in range(PACK):
                    turn(banks[half], i, e[i][:, P * half : P * half + P], False, i == PACK - 1)
                gate = sb("%s%d" % (name, half), [P, N], F32)
                nc.scalar.activation(
                    gate[:].rearrange("v (t p) -> v p t", t=PACK), banks[half][:].rearrange("v (p t) -> v p t", t=PACK), func
                )
                gates.append(gate)
            return gates

        def gather_forget(pre, d, t):
            nc.vector.tensor_tensor(pre[:, t, :], h3[t].indirect(pos_sb[d][:]), e3[t], ALU.add)

        def forget_gate(f, pre):
            for t in range(0, PACK, 2):
                nc.scalar.activation(f[:, t : t + 2, :], pre[:, t : t + 2, :], ACT.Sigmoid)

        def gather_cells(name, f, d, v0, width):
            fc = sb(name, [P, PACK, width], F32)
            picks = pos_sb[d][:, v0 // 16 : (v0 + width) // 16]
            for t in range(PACK):
                nc.vector.tensor_tensor(fc[:, t, :], cell_sb[t][:].indirect(picks), f[:, t, v0 : v0 + width], ALU.mult)
            return fc

        sum_a = [held.tile([P, N], F32, name="sum_a%d" % half) for half in range(2)]
        sum_g = [held.tile([P, N], F32, name="sum_g%d" % half) for half in range(2)]

        x_picked = (sb("xw", [P, S], U32), sb("xs", [P, S], U8))
        nc.vector.tensor_copy(x_picked[0][:], xw_all[:].bitcast(U32).indirect(offs_sb[:]))
        nc.vector.tensor_copy(x_picked[1][:], xs_all[:].indirect(offs_sb[:]))

        for i in range(2):
            stage(on_scalar, "v1", P * i, P * i + P)
            quantize("v1", P * i, P * i + P)
        h1 = child_pair("v1", 0)
        stage(on_vector, "v1", HALF, N)
        quantize("v1", HALF, N)
        stage(on_vector, "v2", 0, HALF)
        stage(on_scalar, "v2", HALF, N)
        gather_children("a", sum_a, 0, h1[0])
        quantize("v2", 0, HALF)
        h1 = h1 + child_pair("v1", 2, "raw_v2_%d" % HALF)
        gather_children("a", sum_a, 1, h1[1])
        quantize("v2", HALF, N)
        stage(on_scalar, "v3", 0, N, deal=True)
        stage(on_vector, "eT", 0, V)
        h2 = child_pair("v2", 0, "raw_v3_0")
        gather_children("a", sum_a, 2, h1[2])
        gather_children("a", sum_a, 3, h1[3])

        quantize("v3", 0, N)
        stage(on_scalar, "w3", 0, N, deal=True)
        gather_children("g", sum_g, 0, h2[0])
        e_codes = quantize("eT", 0, V)
        gather_children("g", sum_g, 1, h2[1])
        stage(on_vector, "w1", 0, N)
        quantize("w3", 0, N)
        h2 = h2 + child_pair("v2", 2, "raw_w3_0")
        e3_banks = [node_pair("w3", i) for i in (0, 2)]
        h3 = [child_block(0), child_block(1)]
        e3 = node_rows("w3", 0, e3_banks[0])
        stage(on_scalar, "w2", 0, N)
        h3.append(child_block(2))
        e3 = e3 + node_rows("w3", 2, e3_banks[1])
        h3.append(child_block(3))
        gather_children("g", sum_g, 2, h2[2])
        gather_children("g", sum_g, 3, h2[3])
        quantize("w1", 0, N)

        pre_first = sb("pre_first", [P, PACK, V], F32)
        gather_forget(pre_first, 0, 0)
        gather_forget(pre_first, 0, 1)
        quantize("w2", 0, N)
        gather_forget(pre_first, 0, 2)
        gather_forget(pre_first, 0, 3)
        e1, e2 = [], []
        for name, e in (("w1", e1), ("w2", e2)):
            for i in (0, 2):
                e.extend(node_rows(name, i, node_pair(name, i)))
        pre_second = sb("pre_second", [P, PACK, V], F32, "raw_w2_0")
        for t in range(PACK):
            gather_forget(pre_second, 1, t)
        f_first = sb("f_first", [P, PACK, V], F32)
        forget_gate(f_first, pre_first)
        a = close_gate("a", sum_a, e1, ACT.Sigmoid)
        g = close_gate("g", sum_g, e2, ACT.Tanh)
        f_second = sb("f_second", [P, PACK, V], F32, "words_w2_0")
        forget_gate(f_second, pre_second)

        total = [held.tile([P, N], F32, name="total%d" % half, tag="bank%d" % (2 + half)) for half in range(2)]
        fc_first = gather_cells("fc_first", f_first, 0, 0, V)
        for half in range(2):
            ag = sb("ag%d" % half, [P, N], F32)
            nc.vector.tensor_tensor(ag[:], a[half][:], g[half][:], ALU.mult)
            for t in range(PACK):
                turn(total[half], t, ag[:, P * t : P * t + P], t == 0, False)
        for half in range(2):
            once = held.tile([P, N], F32, name="once%d" % half, tag="sum_a%d" % half)
            for t in range(PACK):
                turn(once, t, fc_first[:, t, P * half : P * half + P], True, True)
            turned = sb("turned%d" % half, [P, N], F32)
            nc.scalar.copy(out=turned[:], in_=once[:])
            for t in range(PACK):
                turn(total[half], t, turned[:, P * t : P * t + P], False, t == PACK - 1)
        fc_second = [gather_cells("fc_second%d" % half, f_second, 1, P * half, P) for half in range(2)]

        y_words = sb("y_words", [P, V], U32)
        y_scales = sb("y_scales", [P, V], U8)
        for half, copy in enumerate((on_scalar, on_vector)):
            nodes = slice(P * half, P * half + P)
            y = sb("y%d" % half, [P, PACK, P], F32)
            nc.vector.tensor_tensor(
                y[:].rearrange("p t v -> p (t v)"),
                total[half][:],
                fc_second[half][:].rearrange("p t v -> p (t v)"),
                ALU.add,
            )
            nc.sync.dma_start(out=out_0.rearrange("(p t) v -> p t v", t=PACK)[:, :, nodes], in_=y[:])
            y_bf = sb("y_bf%d" % half, [P, P, PACK], BF16)
            interleave(copy, y_bf[:], y[:])
            nc.vector.quantize_mx(
                out=y_words[:, nodes].bitcast(FP8X4),
                scales=y_scales[:, nodes],
                in_=y_bf[:].rearrange("p v t -> p (v t)"),
            )
        nc.sync.dma_start(out=out_1[0].rearrange("p c r -> p (c r)").bitcast(I32), in_=y_words[:].bitcast(I32))
        for q in range(QUADRANTS):
            queue = nc.scalar if q % 2 == 0 else nc.sync
            queue.dma_start(
                out=out_2[0, 4 * q : 4 * q + 4, :].bitcast(I32), in_=y_scales[32 * q : 32 * q + 4, :].bitcast(I32)
            )
